import numpy as np, ml_dtypes
CORES = [26,28,98,100,106,108,122,124]
N = 8
import mx_ref
NC, WT = 256, 1
BF = ml_dtypes.bfloat16
def pk(c, s, i=0):
    return (np.ascontiguousarray(c[:, 512 * i:512 * i + 512]), mx_ref.live(s[:, 128 * i:128 * i + 128]))
def inputs(rng, e, E):
    def f(*shape):
        v = (rng.standard_normal(shape, dtype=np.float32) * np.exp2(rng.integers(-2, 3, shape[:-1] + (1,)))).astype(BF)
        return mx_ref.spread((v.astype(np.float32) * np.exp2(rng.integers(-E, E + 1, shape[:-2] + (1, 1))).astype(np.float32)).astype(BF), rng, e)
    def packed(k):
        c = np.zeros((N, 128, k * 512), np.uint8); s = np.zeros((N, 128, k * 128), np.uint8)
        for r in range(N):
            for i in range(k):
                a, b = mx_ref.quantize(f(128, 512)); c[r][:, 512 * i:512 * i + 512] = a; s[r][:, 128 * i:128 * i + 128] = mx_ref.plane(b, rng)
        return c, s
    d = {}
    d["wc"], d["ws"] = packed(WT)
    d["x"] = f(N, 128, 4 * NC)
    return d
def setup_inputs(rng):
    return inputs(rng, 0, 0)
def setup_inputs_blocks(rng):
    return inputs(rng, 4, 0)
def setup_inputs_wide(rng):
    return inputs(rng, 0, 8)
def reference(wc, ws, x):
    y = np.zeros((N, 128, N * WT * NC), np.float32)
    for r in range(N):
        X = mx_ref.quantize(x[r])
        for b in range(N * WT):
            y[r][:, NC * b:NC * b + NC] = mx_ref.matmul(pk(wc[b // WT], ws[b // WT], b % WT), X)
    return {"y": y}

from concourse.bass import DstId, RemoteDMATransfer
from concourse.mybir import dt, ActivationFunctionType

N = 8
WW = 128
NC = 256
BANK = 512

N_OFF = 8
N_HLP = 8
N_ON = 16

SCRATCH = {
    "wq": ("sbuf", [128, N * WW], "float8_e4m3fn_x4"),
    "wp": ("sbuf", [128, N * WW], "uint8"),
    "xb": ("sbuf", [128, 4 * NC], "bfloat16"),
    "xq": ("sbuf", [128, NC], "float8_e4m3fn_x4"),
    "xp": ("sbuf", [128, NC], "uint8"),
    "ps": ("psum", [128, N * BANK], "float32"),
    "yb": ("sbuf", [128, N * NC], "float32"),
}
for _t in range(N):
    SCRATCH["dq%d" % _t] = ("dram", [128, WW], "float8_e4m3fn_x4")
    SCRATCH["dp%d" % _t] = ("dram", [128, WW], "uint8")
SEMAPHORES = (["ldx", "q", "st", "snt"] + ["mm%d" % i for i in range(N)] + ["cp%d" % i for i in range(N)]
              + [a + b + str(i) for a in "pc" for b in "DS" for i in range(N)])


def _bits(mask):
    return [i for i in range(mask.bit_length()) if (mask >> i) & 1]


def _pow2(n):
    k = 1
    while 2 * k <= n:
        k *= 2
    return k


def _plan(cores, topo):
    chip, die = topo.chip, topo.die
    chips = sorted(set(chip(c) for c in cores))
    at = {x: [c for c in cores if chip(c) == x] for x in chips}
    calls = {c: [] for c in cores}
    lands = {c: [] for c in cores}
    for r, o in enumerate(cores):
        i = chips.index(chip(o))
        far, cut = [], []
        for k in range(1, len(chips)):
            there = at[chips[(i + k) % len(chips)]]
            peers = [d for d in there if die(d) == die(o) and topo.may_write(o, d)]
            if peers:
                far.append(peers[0])
            else:
                cut += there
        idle = [h for h in range(topo.CHIPS * topo.CORES_PER_CHIP)
                if chip(h) == chip(o) and h not in cores and all(topo.may_write(h, d) for d in cut)]
        share = {}
        for d in sorted(cut, key=lambda d: die(d) != die(o)):
            h = min(idle, key=lambda h: (len(share.get(h, [])), die(h) != die(d), h in calls))
            share.setdefault(h, []).append(d)
        first, used = [], []
        if far:
            used = _bits(topo.mask(o, far[0]))[:N_OFF]
            first.append((r, far, used, "D", "D"))
        if share:
            free = [b for b in _bits(topo.mask(o, list(share)[0])) if b not in used]
            first.append((r, list(share), free[:_pow2(min(len(free), N_HLP))], "D", "D"))
        near = [c for c in at[chip(o)] if c != o]
        free = [b for b in _bits(topo.mask(o, near[0])) if b not in used]
        second = [(r, near, free[:_pow2(min(len(free), N_ON))], "S", "S")]
        calls[o] += [("p", first), ("c", first), ("p", second), ("c", second)]
        for h, to in share.items():
            leg = [(r, to, _bits(topo.mask(h, to[0]))[:N_OFF], "D", "S")]
            calls[h] = [("p", leg), ("c", leg)]
        for k, d in enumerate(far):
            lands[d].append((k, r))
    for c in cores:
        lands[c] = [t for _, t in sorted(lands[c])]
        if lands[c]:
            near = [s for s in at[chip(c)] if s != c]
            eng = _bits(topo.mask(c, near[0]))[:N_ON]
            n = _pow2(len(eng) // len(lands[c]))
            calls[c].append(("p", [(t, near, eng[k * n:(k + 1) * n], "D", "S") for k, t in enumerate(lands[c])]))
            calls[c] += [("c", [(t, near, eng, "D", "S")]) for t in lands[c]]
    return calls, lands


def rank_program(g, core, T, topo):
    cores = list(T.cores)
    calls, lands = _plan(cores, topo)
    rank = T.rank_of(core)
    if core not in calls:
        return
    sem = T.sem

    def view(part, place, t):
        if part == "p":
            return T["dp%d" % t][:, :] if place == "D" else T.wp[:, t * WW:(t + 1) * WW]
        return (T["dq%d" % t][:, :] if place == "D" else T.wq[:, t * WW:(t + 1) * WW]).bitcast(dt.uint8)

    here, when = {}, {}
    for src, todo in calls.items():
        for part, group in todo:
            for t, dsts, eng, _, to in group:
                if core in dsts:
                    here[part + to + str(t)] = len(eng)
                    if to == "S":
                        when[t] = (1, 0, 0) if src == cores[t] else (2, lands[src].index(t), 1) if src in cores else (3, dsts.index(core), 0)
    if rank is not None:
        for k, t in enumerate(lands[core]):
            here["pS%d" % t] = here["cS%d" % t] = 16
            when[t] = (2, k, 0)
        for place in "DS":
            for part, q, src in (("p", g.scalar, T.ws[:, 0:WW]), ("c", g.sync, T.wc[:, 0:4 * WW])):
                here[part + place + str(rank)] = 16
                q.dma_start(view(part, place, rank), src).then_inc(sem[part + place + str(rank)], 16)
        g.scalar.dma_start(T.xb[:, :], T.x[:, :]).then_inc(sem.ldx, 16)

    sent = 0
    for part, group in calls[core]:
        transfers = []
        for t, dsts, eng, fr, to in group:
            g.wait_ge(sem[part + fr + str(t)], here[part + fr + str(t)])
            ids = [topo.addr(d) for d in dsts]
            transfers.append(RemoteDMATransfer(
                dst_ids=[DstId(rid=a[0], pnc=a[1]) for a in ids],
                dma_engine_mask=sum(1 << b for b in eng),
                remote_sem=sem[part + to + str(t)],
                srcs=[view(part, fr, t)],
                dsts=[view(part, to, t) for d in dsts]))
            sent += len(eng)
        g.remote_dma_fused(transfers, local_sem=sem.snt)
    g.wait_ge(sem.snt, sent)
    if rank is None:
        return

    g.vector.wait_ge(sem.ldx, 16)
    g.vector.quantize_mx(T.xq[:, :], T.xp[:, :], T.xb[:, :]).then_inc(sem.q, 1)

    order = [rank] + sorted(when, key=lambda t: when[t])
    g.tensor.wait_ge(sem.q, 1)
    for j, t in enumerate(order):
        for part in "pc":
            g.tensor.wait_ge(sem[part + "S" + str(t)], here[part + "S" + str(t)])
        bank = T.ps[:, t * BANK:t * BANK + NC]
        g.tensor.matmul_mx(bank, T.wq[:, t * WW:(t + 1) * WW], T.wp[:, t * WW:(t + 1) * WW], T.xq[:, :], T.xp[:, :],
                           True, True).then_inc(sem["mm%d" % t], 1)
        blk = T.yb[:, t * NC:(t + 1) * NC]
        if j % 2 == 0:
            g.vector.wait_ge(sem["mm%d" % t], 1)
            g.vector.tensor_copy(blk, bank).then_inc(sem["cp%d" % t], 1)
            q = g.sync
        else:
            g.scalar.wait_ge(sem["mm%d" % t], 1)
            g.scalar.activation(blk, bank, ActivationFunctionType.Copy).then_inc(sem["cp%d" % t], 1)
            q = g.scalar
        q.wait_ge(sem["cp%d" % t], 1)
        q.dma_start(T.y[:, t * NC:(t + 1) * NC], blk).then_inc(sem.st, 16)
        if j == 0:
            for part, q in (("p", g.scalar), ("c", g.sync)):
                for u in lands[core]:
                    q.wait_ge(sem[part + "D" + str(u)], here[part + "D" + str(u)])
                    q.dma_start(view(part, "S", u), view(part, "D", u)).then_inc(sem[part + "S" + str(u)], 16)
    g.sync.wait_ge(sem.st, 16 * N)
